import numpy as np, ml_dtypes
CORES = [65,66,69,71,193,194,197,199,321,322,325,327,449,450,453,455]
N = 16
KB, QP = 2, 256
MEM = [0]
def setup_inputs(rng):
    return {"q": rng.standard_normal((N, 128, QP), dtype=np.float32).astype(ml_dtypes.bfloat16), "k": rng.standard_normal((N, 128, KB * 128), dtype=np.float32).astype(ml_dtypes.bfloat16), "v": rng.standard_normal((N, 128, KB * 128), dtype=np.float32).astype(ml_dtypes.bfloat16)}
def setup_inputs_big(rng):
    d = setup_inputs(rng)
    for k in ("q", "k", "v"): d[k] = (d[k].astype(np.float32) * 1024.0).astype(d[k].dtype)
    return d
def setup_inputs_small(rng):
    d = setup_inputs(rng)
    for k in ("q", "k", "v"): d[k] = (d[k].astype(np.float32) * (1 / 1024.0)).astype(d[k].dtype)
    return d
def setup_inputs_apart(rng):
    d = setup_inputs(rng)
    f = (10.0 ** rng.permutation(np.linspace(-1.5, 1.5, N))).astype(np.float32).reshape(N, 1, 1)
    for k in ("q", "k", "v"): d[k] = (d[k].astype(np.float32) * f).astype(d[k].dtype)
    return d
def reference(q, k, v):
    Q, K, V = q.astype(np.float64), k.astype(np.float64), v.astype(np.float64)
    y = np.zeros((N, 128, QP))
    for r in range(N):
        for j in MEM:
            for b in range(KB):
                S = np.maximum(K[j][:, 128 * b:128 * b + 128].T @ Q[r], 0.0)
                y[r] += V[j][:, 128 * b:128 * b + 128].T @ S
    return {"y": y.astype(ml_dtypes.bfloat16 if q.dtype != np.float64 else np.float64)}

@@ -1,0 +1,158 @@
+from concourse.bass import DstId, RemoteDMATransfer
+from concourse.mybir import AluOpType
+
+SCRATCH = {
+    "kvd": ("dram", [128, 512], "bfloat16"),
+    "kv": ("sbuf", [128, 512], "bfloat16"),
+    "qs": ("sbuf", [128, 256], "bfloat16"),
+    "zero": ("sbuf", [128, 256], "float32"),
+    "s0": ("sbuf", [128, 256], "bfloat16"),
+    "s1": ("sbuf", [128, 256], "bfloat16"),
+    "ys": ("sbuf", [128, 256], "bfloat16"),
+    "ps0": ("psum", [128, 512], "float32"),
+    "ps1": ("psum", [128, 512], "float32"),
+    "po": ("psum", [128, 512], "float32"),
+}
+SEMAPHORES = ["ld", "ld2", "lq", "arr", "sent", "zs", "mm0", "mm1", "rl0", "rl1", "mo", "cp", "st"]
+
+
+def _bits(mask):
+    return [i for i in range(mask.bit_length()) if (mask >> i) & 1]
+
+
+def _mask(engines):
+    m = 0
+    for e in engines:
+        m |= 1 << e
+    return m
+
+
+def _same_chip(topo, a, b):
+    return topo.host(a) == topo.host(b) and topo.chip(a) == topo.chip(b)
+
+
+def _tree(T, topo):
+    cores = list(T.cores)
+    root = cores[T.tables["MEM"][0]]
+    by_host = {}
+    for c in cores:
+        by_host.setdefault(topo.host(c), []).append(c)
+    home = by_host[topo.host(root)]
+    pos = home.index(root)
+    others = [h for h in by_host if h != topo.host(root)]
+    near = [h for h in others if topo.may_write(root, by_host[h][pos])]
+    far = [h for h in others if h not in near]
+    gates = [by_host[h][pos] for h in near]
+    peers = [c for c in home if c != root]
+    children = {c: [] for c in cores}
+    children[root] = gates + peers
+    for p in peers:
+        children[p] = [by_host[h][home.index(p)] for h in near]
+    for h in far:
+        leaves = list(by_host[h])
+        gs = [x for x in gates if topo.may_write(x, leaves[0])]
+        gs.sort(key=lambda x: 0 if topo.same_plane(x, leaves[0]) else 1)
+        leaves.sort(key=lambda c: 0 if topo.die(c) == topo.die(gs[0]) else 1)
+        share = len(leaves) // len(gs)
+        for i, x in enumerate(gs):
+            children[x] = children[x] + leaves[i * share:(i + 1) * share]
+    level = {root: 0}
+    for c in children[root]:
+        level[c] = 1
+        for d in children[c]:
+            level[d] = 2
+    return root, children, level
+
+
+def _send(g, core, T, topo, kids, dst_of):
+    off = [d for d in kids if not _same_chip(topo, core, d)]
+    on = [d for d in kids if _same_chip(topo, core, d)]
+    transfers, gets, total = [], {}, 0
+    off_eng = _bits(topo.mask(core, off[0])) if off else []
+    for j, d in enumerate(off):
+        eng = off_eng[j::len(off)]
+        rid, pid = topo.addr(d, core)
+        transfers.append(RemoteDMATransfer(dst_ids=[DstId(rid=rid, pnc=pid)], dma_engine_mask=_mask(eng),
+                                           remote_sem=T.sem.arr, src=T.kvd[:], dst=dst_of(d)))
+        gets[d] = len(eng)
+        total += len(eng)
+    if on:
+        eng = [e for e in _bits(topo.mask(core, on[0])) if e not in off_eng]
+        ids = []
+        for d in on:
+            rid, pid = topo.addr(d, core)
+            ids.append(DstId(rid=rid, pnc=pid))
+            gets[d] = len(eng)
+        transfers.append(RemoteDMATransfer(dst_ids=ids, dma_engine_mask=_mask(eng), remote_sem=T.sem.arr,
+                                           srcs=[T.kvd[:]], dsts=[dst_of(d) for d in on]))
+        total += len(eng)
+    g.remote_dma_fused(transfers, local_sem=T.sem.sent)
+    return gets, total
+
+
+def _arrival(core, T, topo, parent, kids):
+    off = [d for d in kids if not _same_chip(topo, parent, d)]
+    on = [d for d in kids if _same_chip(topo, parent, d)]
+    off_eng = _bits(topo.mask(parent, off[0])) if off else []
+    if core in off:
+        return len(off_eng[off.index(core)::len(off)])
+    return len([e for e in _bits(topo.mask(parent, on[0])) if e not in off_eng])
+
+
+def rank_program(g, core, T, topo):
+    if T.rank_of(core) is None:
+        return
+    sem = T.sem
+    root, children, level = _tree(T, topo)
+    lev = level[core]
+    kids = children[core]
+    parent = None
+    for c in children:
+        if core in children[c]:
+            parent = c
+
+    g.vector.memset(T.zero[:], 0.0).then_inc(sem.zs, 1)
+
+    if lev == 0:
+        g.sync.dma_start(T.kvd[:, 0:256], T.k[:]).then_inc(sem.ld, 16)
+        g.scalar.dma_start(T.kvd[:, 256:512], T.v[:]).then_inc(sem.ld, 16)
+        g.sync.dma_start(T.kv[:, 0:256], T.k[:]).then_inc(sem.ld2, 16)
+        g.scalar.dma_start(T.kv[:, 256:512], T.v[:]).then_inc(sem.ld2, 16)
+        g.sync.dma_start(T.qs[:], T.q[:]).then_inc(sem.lq, 16)
+        g.wait_ge(sem.ld, 32)
+        _, total = _send(g, core, T, topo, kids, lambda d: T.kvd[:])
+        g.tensor.wait_ge(sem.ld2, 32)
+    elif lev == 1:
+        n = _arrival(core, T, topo, parent, children[parent])
+        g.sync.dma_start(T.qs[:], T.q[:]).then_inc(sem.lq, 16)
+        g.wait_ge(sem.arr, n)
+        _, total = _send(g, core, T, topo, kids, lambda d: T.kv[:])
+        g.sync.wait_ge(sem.arr, n)
+        g.sync.dma_start(T.kv[:], T.kvd[:]).then_inc(sem.ld2, 16)
+        g.tensor.wait_ge(sem.ld2, 16)
+    else:
+        n = _arrival(core, T, topo, parent, children[parent])
+        total = 0
+        g.sync.dma_start(T.qs[:], T.q[:]).then_inc(sem.lq, 16)
+        g.tensor.wait_ge(sem.arr, n)
+
+    te, ve = g.tensor, g.vector
+    te.wait_ge(sem.lq, 16)
+    te.matmul(T.ps0[:, 0:256], T.kv[:, 0:128], T.qs[:], start=True, stop=True).then_inc(sem.mm0, 1)
+    te.matmul(T.ps1[:, 0:256], T.kv[:, 128:256], T.qs[:], start=True, stop=True).then_inc(sem.mm1, 1)
+    ve.wait_ge(sem.zs, 1)
+    ve.wait_ge(sem.mm0, 1)
+    ve.tensor_tensor(T.s0[:], T.ps0[:, 0:256], T.zero[:], AluOpType.max).then_inc(sem.rl0, 1)
+    ve.wait_ge(sem.mm1, 1)
+    ve.tensor_tensor(T.s1[:], T.ps1[:, 0:256], T.zero[:], AluOpType.max).then_inc(sem.rl1, 1)
+    te.wait_ge(sem.rl0, 1)
+    te.matmul(T.po[:, 0:256], T.kv[:, 256:384], T.s0[:], start=True, stop=False)
+    te.wait_ge(sem.rl1, 1)
+    te.matmul(T.po[:, 0:256], T.kv[:, 384:512], T.s1[:], start=False, stop=True).then_inc(sem.mo, 1)
+    ve.wait_ge(sem.mo, 1)
+    ve.tensor_copy(T.ys[:], T.po[:, 0:256]).then_inc(sem.cp, 1)
+    g.sync.wait_ge(sem.cp, 1)
+    g.sync.dma_start(T.y[:], T.ys[:]).then_inc(sem.st, 16)
+    g.sync.wait_ge(sem.st, 16)
+    if total:
+        g.wait_ge(sem.sent, total)

@@ -1,8 +1,14 @@
 from concourse.bass import DstId, RemoteDMATransfer
 from concourse.mybir import AluOpType
 
+CHUNK = True
+L1_DRAM = True
+ROOT_OFF, ROOT_ON, FWD_OFF = 4, 8, 4
+
 SCRATCH = {
     "kvd": ("dram", [128, 512], "bfloat16"),
+    "kd": ("dram", [128, 256], "bfloat16"),
+    "vd": ("dram", [128, 256], "bfloat16"),
     "kv": ("sbuf", [128, 512], "bfloat16"),
     "qs": ("sbuf", [128, 256], "bfloat16"),
     "zero": ("sbuf", [128, 256], "float32"),
@@ -13,7 +19,8 @@ SCRATCH = {
     "ps1": ("psum", [128, 512], "float32"),
     "po": ("psum", [128, 512], "float32"),
 }
-SEMAPHORES = ["ld", "ld2", "lq", "arr", "sent", "zs", "mm0", "mm1", "rl0", "rl1", "mo", "cp", "st"]
+SEMAPHORES = ["ld0", "ld1", "own0", "own1", "lq", "arr0", "arr1", "sent", "zs", "mm0", "mm1", "rl0", "rl1", "mo", "cp",
+              "st"]
 
 
 def _bits(mask):
@@ -64,39 +71,40 @@ def _tree(T, topo):
     return root, children, level
 
 
-def _send(g, core, T, topo, kids, dst_of):
-    off = [d for d in kids if not _same_chip(topo, core, d)]
-    on = [d for d in kids if _same_chip(topo, core, d)]
-    transfers, gets, total = [], {}, 0
-    off_eng = _bits(topo.mask(core, off[0])) if off else []
+def _shares(topo, src, kids, n_off, n_on):
+    off = [d for d in kids if not _same_chip(topo, src, d)]
+    on = [d for d in kids if _same_chip(topo, src, d)]
+    off_eng = _bits(topo.mask(src, off[0])) if off else []
+    sh = {}
     for j, d in enumerate(off):
-        eng = off_eng[j::len(off)]
-        rid, pid = topo.addr(d, core)
-        transfers.append(RemoteDMATransfer(dst_ids=[DstId(rid=rid, pnc=pid)], dma_engine_mask=_mask(eng),
-                                           remote_sem=T.sem.arr, src=T.kvd[:], dst=dst_of(d)))
-        gets[d] = len(eng)
-        total += len(eng)
-    if on:
-        eng = [e for e in _bits(topo.mask(core, on[0])) if e not in off_eng]
+        mine = off_eng[j::len(off)]
+        sh[d] = mine[::len(mine) // n_off]
+    for d in on:
+        mine = [e for e in _bits(topo.mask(src, d)) if e not in off_eng]
+        sh[d] = mine[::len(mine) // n_on]
+    return sh
+
+
+def _send(g, core, T, topo, kids, sh, src, dst, rsem):
+    groups = []
+    for d in kids:
+        for grp in groups:
+            if sh[grp[0]] == sh[d]:
+                grp.append(d)
+                break
+        else:
+            groups.append([d])
+    transfers, total = [], 0
+    for grp in groups:
         ids = []
-        for d in on:
+        for d in grp:
             rid, pid = topo.addr(d, core)
             ids.append(DstId(rid=rid, pnc=pid))
-            gets[d] = len(eng)
-        transfers.append(RemoteDMATransfer(dst_ids=ids, dma_engine_mask=_mask(eng), remote_sem=T.sem.arr,
-                                           srcs=[T.kvd[:]], dsts=[dst_of(d) for d in on]))
-        total += len(eng)
+        transfers.append(RemoteDMATransfer(dst_ids=ids, dma_engine_mask=_mask(sh[grp[0]]), remote_sem=rsem,
+                                           srcs=[src], dsts=[dst for d in grp]))
+        total += len(sh[grp[0]])
     g.remote_dma_fused(transfers, local_sem=T.sem.sent)
-    return gets, total
-
-
-def _arrival(core, T, topo, parent, kids):
-    off = [d for d in kids if not _same_chip(topo, parent, d)]
-    on = [d for d in kids if _same_chip(topo, parent, d)]
-    off_eng = _bits(topo.mask(parent, off[0])) if off else []
-    if core in off:
-        return len(off_eng[off.index(core)::len(off)])
-    return len([e for e in _bits(topo.mask(parent, on[0])) if e not in off_eng])
+    return total
 
 
 def rank_program(g, core, T, topo):
@@ -111,33 +119,64 @@ def rank_program(g, core, T, topo):
         if core in children[c]:
             parent = c
 
-    g.vector.memset(T.zero[:], 0.0).then_inc(sem.zs, 1)
+    def shares_of(c):
+        if level[c] == 0:
+            return _shares(topo, c, children[c], ROOT_OFF, ROOT_ON)
+        return _shares(topo, c, children[c], FWD_OFF, FWD_OFF)
 
-    if lev == 0:
-        g.sync.dma_start(T.kvd[:, 0:256], T.k[:]).then_inc(sem.ld, 16)
-        g.scalar.dma_start(T.kvd[:, 256:512], T.v[:]).then_inc(sem.ld, 16)
-        g.sync.dma_start(T.kv[:, 0:256], T.k[:]).then_inc(sem.ld2, 16)
-        g.scalar.dma_start(T.kv[:, 256:512], T.v[:]).then_inc(sem.ld2, 16)
-        g.sync.dma_start(T.qs[:], T.q[:]).then_inc(sem.lq, 16)
-        g.wait_ge(sem.ld, 32)
-        _, total = _send(g, core, T, topo, kids, lambda d: T.kvd[:])
-        g.tensor.wait_ge(sem.ld2, 32)
-    elif lev == 1:
-        n = _arrival(core, T, topo, parent, children[parent])
-        g.sync.dma_start(T.qs[:], T.q[:]).then_inc(sem.lq, 16)
-        g.wait_ge(sem.arr, n)
-        _, total = _send(g, core, T, topo, kids, lambda d: T.kv[:])
-        g.sync.wait_ge(sem.arr, n)
-        g.sync.dma_start(T.kv[:], T.kvd[:]).then_inc(sem.ld2, 16)
-        g.tensor.wait_ge(sem.ld2, 16)
+    if CHUNK:
+        pieces = [(T.kd[:], T.kv[:, 0:256]), (T.vd[:], T.kv[:, 256:512])]
     else:
-        n = _arrival(core, T, topo, parent, children[parent])
-        total = 0
+        pieces = [(T.kvd[:], T.kv[:])]
+    P = len(pieces)
+    queues = [g.sync, g.scalar]
+
+    g.vector.memset(T.zero[:], 0.0).then_inc(sem.zs, 1)
+    total = 0
+    if lev == 0:
+        own = [(sem["own%d" % i], 32 // P) for i in range(P)]
+        if L1_DRAM:
+            if CHUNK:
+                g.sync.dma_start(T.kd[:], T.k[:]).then_inc(sem.ld0, 16)
+                g.scalar.dma_start(T.vd[:], T.v[:]).then_inc(sem.ld1, 16)
+            else:
+                g.sync.dma_start(T.kvd[:, 0:256], T.k[:]).then_inc(sem.ld0, 16)
+                g.scalar.dma_start(T.kvd[:, 256:512], T.v[:]).then_inc(sem.ld0, 16)
+        g.sync.dma_start(T.kv[:, 0:256], T.k[:]).then_inc(sem.own0, 16)
+        g.scalar.dma_start(T.kv[:, 256:512], T.v[:]).then_inc(sem["own%d" % (P - 1)], 16)
         g.sync.dma_start(T.qs[:], T.q[:]).then_inc(sem.lq, 16)
-        g.tensor.wait_ge(sem.arr, n)
+        sh = shares_of(core)
+        for i in range(P):
+            if L1_DRAM:
+                g.wait_ge(sem["ld%d" % i], 32 // P)
+            else:
+                g.wait_ge(own[i][0], own[i][1])
+            side = pieces[i][0] if L1_DRAM else pieces[i][1]
+            total += _send(g, core, T, topo, kids, sh, side, side, sem["arr%d" % i])
+        ready = own
+    elif lev == 1:
+        n = len(shares_of(parent)[core])
+        g.sync.dma_start(T.qs[:], T.q[:]).then_inc(sem.lq, 16)
+        sh = shares_of(core)
+        for i in range(P):
+            g.wait_ge(sem["arr%d" % i], n)
+            side = pieces[i][0] if L1_DRAM else pieces[i][1]
+            total += _send(g, core, T, topo, kids, sh, side, pieces[i][1], sem["arr%d" % i])
+        if L1_DRAM:
+            for i in range(P):
+                queues[i].wait_ge(sem["arr%d" % i], n)
+                queues[i].dma_start(pieces[i][1], pieces[i][0]).then_inc(sem["own%d" % i], 16)
+            ready = [(sem["own%d" % i], 16) for i in range(P)]
+        else:
+            ready = [(sem["arr%d" % i], n) for i in range(P)]
+    else:
+        n = len(shares_of(parent)[core])
+        g.sync.dma_start(T.qs[:], T.q[:]).then_inc(sem.lq, 16)
+        ready = [(sem["arr%d" % i], n) for i in range(P)]
 
     te, ve = g.tensor, g.vector
     te.wait_ge(sem.lq, 16)
+    te.wait_ge(ready[0][0], ready[0][1])
     te.matmul(T.ps0[:, 0:256], T.kv[:, 0:128], T.qs[:], start=True, stop=True).then_inc(sem.mm0, 1)
     te.matmul(T.ps1[:, 0:256], T.kv[:, 128:256], T.qs[:], start=True, stop=True).then_inc(sem.mm1, 1)
     ve.wait_ge(sem.zs, 1)
@@ -145,6 +184,8 @@ def rank_program(g, core, T, topo):
     ve.tensor_tensor(T.s0[:], T.ps0[:, 0:256], T.zero[:], AluOpType.max).then_inc(sem.rl0, 1)
     ve.wait_ge(sem.mm1, 1)
     ve.tensor_tensor(T.s1[:], T.ps1[:, 0:256], T.zero[:], AluOpType.max).then_inc(sem.rl1, 1)
+    if P > 1:
+        te.wait_ge(ready[1][0], ready[1][1])
     te.wait_ge(sem.rl0, 1)
     te.matmul(T.po[:, 0:256], T.kv[:, 256:384], T.s0[:], start=True, stop=False)
     te.wait_ge(sem.rl1, 1)

@@ -1,15 +1,12 @@
 from concourse.bass import DstId, RemoteDMATransfer
 from concourse.mybir import AluOpType
 
-CHUNK = True
-L1_DRAM = True
-ROOT_OFF, ROOT_ON, FWD_OFF = 4, 8, 4
+NP = 4
+W = 128
 
 SCRATCH = {
-    "kvd": ("dram", [128, 512], "bfloat16"),
-    "kd": ("dram", [128, 256], "bfloat16"),
-    "vd": ("dram", [128, 256], "bfloat16"),
-    "kv": ("sbuf", [128, 512], "bfloat16"),
+    "pd": ("dram", [NP, 128, W], "bfloat16"),
+    "kv": ("sbuf", [128, NP * W], "bfloat16"),
     "qs": ("sbuf", [128, 256], "bfloat16"),
     "zero": ("sbuf", [128, 256], "float32"),
     "s0": ("sbuf", [128, 256], "bfloat16"),
@@ -19,8 +16,8 @@ SCRATCH = {
     "ps1": ("psum", [128, 512], "float32"),
     "po": ("psum", [128, 512], "float32"),
 }
-SEMAPHORES = ["ld0", "ld1", "own0", "own1", "lq", "arr0", "arr1", "sent", "zs", "mm0", "mm1", "rl0", "rl1", "mo", "cp",
-              "st"]
+SEMAPHORES = ["ld0", "ld1", "own0", "own1", "lq", "arr0", "arr1", "arr2", "arr3", "sent", "zs", "mm0", "mm1", "rl0",
+              "rl1", "mo", "cp", "st"]
 
 
 def _bits(mask):
@@ -34,162 +31,125 @@ def _mask(engines):
     return m
 
 
-def _same_chip(topo, a, b):
-    return topo.host(a) == topo.host(b) and topo.chip(a) == topo.chip(b)
-
-
-def _tree(T, topo):
+def _plan(T, topo):
     cores = list(T.cores)
     root = cores[T.tables["MEM"][0]]
     by_host = {}
     for c in cores:
         by_host.setdefault(topo.host(c), []).append(c)
-    home = by_host[topo.host(root)]
-    pos = home.index(root)
+    peers = [c for c in by_host[topo.host(root)] if c != root]
     others = [h for h in by_host if h != topo.host(root)]
-    near = [h for h in others if topo.may_write(root, by_host[h][pos])]
-    far = [h for h in others if h not in near]
-    gates = [by_host[h][pos] for h in near]
-    peers = [c for c in home if c != root]
-    children = {c: [] for c in cores}
-    children[root] = gates + peers
-    for p in peers:
-        children[p] = [by_host[h][home.index(p)] for h in near]
-    for h in far:
-        leaves = list(by_host[h])
-        gs = [x for x in gates if topo.may_write(x, leaves[0])]
-        gs.sort(key=lambda x: 0 if topo.same_plane(x, leaves[0]) else 1)
-        leaves.sort(key=lambda c: 0 if topo.die(c) == topo.die(gs[0]) else 1)
-        share = len(leaves) // len(gs)
-        for i, x in enumerate(gs):
-            children[x] = children[x] + leaves[i * share:(i + 1) * share]
-    level = {root: 0}
-    for c in children[root]:
-        level[c] = 1
-        for d in children[c]:
-            level[d] = 2
-    return root, children, level
+    near_h = [h for h in others if topo.may_write(root, by_host[h][0])]
+    far_h = [h for h in others if h not in near_h]
+    near = []
+    for h in near_h:
+        first, second, seen = [], [], []
+        for c in by_host[h]:
+            if topo.die(c) in seen:
+                second.append(c)
+            else:
+                seen.append(topo.die(c))
+                first.append(c)
+        near.append(first + second)
+    far_of = {}
+    for h in far_h:
+        leaves = by_host[h]
+        share = len(leaves) // len(near)
+        for i, gates in enumerate(near):
+            for x in gates:
+                far_of[x] = leaves[i * share:(i + 1) * share]
+    return root, peers, near, far_of
 
 
-def _shares(topo, src, kids, n_off, n_on):
-    off = [d for d in kids if not _same_chip(topo, src, d)]
-    on = [d for d in kids if _same_chip(topo, src, d)]
-    off_eng = _bits(topo.mask(src, off[0])) if off else []
-    sh = {}
-    for j, d in enumerate(off):
-        mine = off_eng[j::len(off)]
-        sh[d] = mine[::len(mine) // n_off]
-    for d in on:
-        mine = [e for e in _bits(topo.mask(src, d)) if e not in off_eng]
-        sh[d] = mine[::len(mine) // n_on]
-    return sh
-
-
-def _send(g, core, T, topo, kids, sh, src, dst, rsem):
-    groups = []
-    for d in kids:
-        for grp in groups:
-            if sh[grp[0]] == sh[d]:
-                grp.append(d)
-                break
-        else:
-            groups.append([d])
-    transfers, total = [], 0
-    for grp in groups:
-        ids = []
-        for d in grp:
-            rid, pid = topo.addr(d, core)
-            ids.append(DstId(rid=rid, pnc=pid))
-        transfers.append(RemoteDMATransfer(dst_ids=ids, dma_engine_mask=_mask(sh[grp[0]]), remote_sem=rsem,
-                                           srcs=[src], dsts=[dst for d in grp]))
-        total += len(sh[grp[0]])
-    g.remote_dma_fused(transfers, local_sem=T.sem.sent)
-    return total
+def _xfer(topo, core, dsts, engines, rsem, src, dst):
+    ids = []
+    for d in dsts:
+        rid, pid = topo.addr(d, core)
+        ids.append(DstId(rid=rid, pnc=pid))
+    return RemoteDMATransfer(dst_ids=ids, dma_engine_mask=_mask(engines), remote_sem=rsem, srcs=[src],
+                             dsts=[dst for d in dsts])
 
 
 def rank_program(g, core, T, topo):
     if T.rank_of(core) is None:
         return
     sem = T.sem
-    root, children, level = _tree(T, topo)
-    lev = level[core]
-    kids = children[core]
-    parent = None
-    for c in children:
-        if core in children[c]:
-            parent = c
+    root, peers, near, far_of = _plan(T, topo)
+    arr = [sem["arr%d" % i] for i in range(NP)]
+    col = [T.kv[:, i * W:(i + 1) * W] for i in range(NP)]
 
-    def shares_of(c):
-        if level[c] == 0:
-            return _shares(topo, c, children[c], ROOT_OFF, ROOT_ON)
-        return _shares(topo, c, children[c], FWD_OFF, FWD_OFF)
-
-    if CHUNK:
-        pieces = [(T.kd[:], T.kv[:, 0:256]), (T.vd[:], T.kv[:, 256:512])]
-    else:
-        pieces = [(T.kvd[:], T.kv[:])]
-    P = len(pieces)
-    queues = [g.sync, g.scalar]
+    out = _bits(topo.mask(root, near[0][0]))
+    stay = [e for e in _bits(topo.mask(root, peers[0])) if e not in out]
+    nt = 2 * len(near)
+    root_eng = [out[j::nt] for j in range(nt)]
+    gate_far = [out[0::4], out[2::4]]
+    gate_on = out[1::2]
 
     g.vector.memset(T.zero[:], 0.0).then_inc(sem.zs, 1)
     total = 0
-    if lev == 0:
-        own = [(sem["own%d" % i], 32 // P) for i in range(P)]
-        if L1_DRAM:
-            if CHUNK:
-                g.sync.dma_start(T.kd[:], T.k[:]).then_inc(sem.ld0, 16)
-                g.scalar.dma_start(T.vd[:], T.v[:]).then_inc(sem.ld1, 16)
-            else:
-                g.sync.dma_start(T.kvd[:, 0:256], T.k[:]).then_inc(sem.ld0, 16)
-                g.scalar.dma_start(T.kvd[:, 256:512], T.v[:]).then_inc(sem.ld0, 16)
-        g.sync.dma_start(T.kv[:, 0:256], T.k[:]).then_inc(sem.own0, 16)
-        g.scalar.dma_start(T.kv[:, 256:512], T.v[:]).then_inc(sem["own%d" % (P - 1)], 16)
+    if core == root:
+        g.sync.dma_start(T.pd[0], T.k[:, 0:W]).then_inc(sem.ld0, 16)
+        g.scalar.dma_start(T.pd[1], T.k[:, W:2 * W]).then_inc(sem.ld0, 16)
+        g.sync.dma_start(T.pd[2], T.v[:, 0:W]).then_inc(sem.ld1, 16)
+        g.scalar.dma_start(T.pd[3], T.v[:, W:2 * W]).then_inc(sem.ld1, 16)
+        g.sync.dma_start(T.kv[:, 0:2 * W], T.k[:]).then_inc(sem.own0, 16)
+        g.scalar.dma_start(T.kv[:, 2 * W:4 * W], T.v[:]).then_inc(sem.own1, 16)
         g.sync.dma_start(T.qs[:], T.q[:]).then_inc(sem.lq, 16)
-        sh = shares_of(core)
-        for i in range(P):
-            if L1_DRAM:
-                g.wait_ge(sem["ld%d" % i], 32 // P)
-            else:
-                g.wait_ge(own[i][0], own[i][1])
-            side = pieces[i][0] if L1_DRAM else pieces[i][1]
-            total += _send(g, core, T, topo, kids, sh, side, side, sem["arr%d" % i])
-        ready = own
-    elif lev == 1:
-        n = len(shares_of(parent)[core])
+        for half, ld in ((0, sem.ld0), (1, sem.ld1)):
+            g.wait_ge(ld, 32)
+            transfers = []
+            for i in (2 * half, 2 * half + 1):
+                for gates in near:
+                    eng = root_eng[len(transfers)]
+                    transfers.append(_xfer(topo, core, [gates[i]], eng, arr[i], T.pd[i], T.pd[i]))
+                    total += len(eng)
+            g.remote_dma_fused(transfers, local_sem=sem.sent)
+        g.wait_ge(sem.own0, 16)
+        g.wait_ge(sem.own1, 16)
+        g.remote_dma_fused([_xfer(topo, core, peers, stay, arr[0], T.kv[:], T.kv[:])], local_sem=sem.sent)
+        total += len(stay)
+        ready = [(sem.own0, 16), (sem.own0, 16), (sem.own1, 16), (sem.own1, 16)]
+    elif core in peers:
         g.sync.dma_start(T.qs[:], T.q[:]).then_inc(sem.lq, 16)
-        sh = shares_of(core)
-        for i in range(P):
-            g.wait_ge(sem["arr%d" % i], n)
-            side = pieces[i][0] if L1_DRAM else pieces[i][1]
-            total += _send(g, core, T, topo, kids, sh, side, pieces[i][1], sem["arr%d" % i])
-        if L1_DRAM:
-            for i in range(P):
-                queues[i].wait_ge(sem["arr%d" % i], n)
-                queues[i].dma_start(pieces[i][1], pieces[i][0]).then_inc(sem["own%d" % i], 16)
-            ready = [(sem["own%d" % i], 16) for i in range(P)]
-        else:
-            ready = [(sem["arr%d" % i], n) for i in range(P)]
+        ready = [(arr[0], len(stay))] * NP
+    elif core in far_of:
+        gates = [gs for gs in near if core in gs][0]
+        me = gates.index(core)
+        n = len(root_eng[0])
+        g.sync.dma_start(T.qs[:], T.q[:]).then_inc(sem.lq, 16)
+        g.wait_ge(arr[me], n)
+        transfers = [_xfer(topo, core, [d], gate_far[j], arr[me], T.pd[me], col[me])
+                     for j, d in enumerate(far_of[core])]
+        transfers.append(_xfer(topo, core, [c for c in gates if c != core], gate_on, arr[me], T.pd[me], col[me]))
+        g.remote_dma_fused(transfers, local_sem=sem.sent)
+        total = sum(len(gate_far[j]) for j in range(len(far_of[core]))) + len(gate_on)
+        g.sync.wait_ge(arr[me], n)
+        g.sync.dma_start(col[me], T.pd[me]).then_inc(sem.own0, 16)
+        ready = [(arr[i], len(gate_on)) for i in range(NP)]
+        ready[me] = (sem.own0, 16)
     else:
-        n = len(shares_of(parent)[core])
+        feeders = [x for x in far_of if core in far_of[x]]
+        j = far_of[feeders[0]].index(core)
         g.sync.dma_start(T.qs[:], T.q[:]).then_inc(sem.lq, 16)
-        ready = [(sem["arr%d" % i], n) for i in range(P)]
+        ready = [(arr[i], len(gate_far[j])) for i in range(NP)]
 
     te, ve = g.tensor, g.vector
     te.wait_ge(sem.lq, 16)
     te.wait_ge(ready[0][0], ready[0][1])
-    te.matmul(T.ps0[:, 0:256], T.kv[:, 0:128], T.qs[:], start=True, stop=True).then_inc(sem.mm0, 1)
-    te.matmul(T.ps1[:, 0:256], T.kv[:, 128:256], T.qs[:], start=True, stop=True).then_inc(sem.mm1, 1)
+    te.matmul(T.ps0[:, 0:256], col[0], T.qs[:], start=True, stop=True).then_inc(sem.mm0, 1)
+    te.wait_ge(ready[1][0], ready[1][1])
+    te.matmul(T.ps1[:, 0:256], col[1], T.qs[:], start=True, stop=True).then_inc(sem.mm1, 1)
     ve.wait_ge(sem.zs, 1)
     ve.wait_ge(sem.mm0, 1)
     ve.tensor_tensor(T.s0[:], T.ps0[:, 0:256], T.zero[:], AluOpType.max).then_inc(sem.rl0, 1)
     ve.wait_ge(sem.mm1, 1)
     ve.tensor_tensor(T.s1[:], T.ps1[:, 0:256], T.zero[:], AluOpType.max).then_inc(sem.rl1, 1)
-    if P > 1:
-        te.wait_ge(ready[1][0], ready[1][1])
+    te.wait_ge(ready[2][0], ready[2][1])
     te.wait_ge(sem.rl0, 1)
-    te.matmul(T.po[:, 0:256], T.kv[:, 256:384], T.s0[:], start=True, stop=False)
+    te.matmul(T.po[:, 0:256], col[2], T.s0[:], start=True, stop=False)
+    te.wait_ge(ready[3][0], ready[3][1])
     te.wait_ge(sem.rl1, 1)
-    te.matmul(T.po[:, 0:256], T.kv[:, 384:512], T.s1[:], start=False, stop=True).then_inc(sem.mo, 1)
+    te.matmul(T.po[:, 0:256], col[3], T.s1[:], start=False, stop=True).then_inc(sem.mo, 1)
     ve.wait_ge(sem.mo, 1)
     ve.tensor_copy(T.ys[:], T.po[:, 0:256]).then_inc(sem.cp, 1)
     g.sync.wait_ge(sem.cp, 1)

@@ -1,12 +1,9 @@
 from concourse.bass import DstId, RemoteDMATransfer
 from concourse.mybir import AluOpType
 
-NP = 4
-W = 128
-
 SCRATCH = {
-    "pd": ("dram", [NP, 128, W], "bfloat16"),
-    "kv": ("sbuf", [128, NP * W], "bfloat16"),
+    "pd": ("dram", [8, 128, 64], "bfloat16"),
+    "kv": ("sbuf", [128, 512], "bfloat16"),
     "qs": ("sbuf", [128, 256], "bfloat16"),
     "zero": ("sbuf", [128, 256], "float32"),
     "s0": ("sbuf", [128, 256], "bfloat16"),
@@ -16,8 +13,8 @@ SCRATCH = {
     "ps1": ("psum", [128, 512], "float32"),
     "po": ("psum", [128, 512], "float32"),
 }
-SEMAPHORES = ["ld0", "ld1", "own0", "own1", "lq", "arr0", "arr1", "arr2", "arr3", "sent", "zs", "mm0", "mm1", "rl0",
-              "rl1", "mo", "cp", "st"]
+SEMAPHORES = ["ld0", "ld1", "own0", "own1", "lq", "g0", "g1", "a0", "a1", "sent", "zs", "mm0", "mm1", "rl0", "rl1",
+              "mo", "cp", "st"]
 
 
 def _bits(mask):
@@ -41,23 +38,19 @@ def _plan(T, topo):
     others = [h for h in by_host if h != topo.host(root)]
     near_h = [h for h in others if topo.may_write(root, by_host[h][0])]
     far_h = [h for h in others if h not in near_h]
-    near = []
-    for h in near_h:
-        first, second, seen = [], [], []
-        for c in by_host[h]:
-            if topo.die(c) in seen:
-                second.append(c)
-            else:
-                seen.append(topo.die(c))
-                first.append(c)
-        near.append(first + second)
-    far_of = {}
+    near = [by_host[h] for h in near_h]
+    far_of = {x: [] for gates in near for x in gates}
     for h in far_h:
         leaves = by_host[h]
-        share = len(leaves) // len(near)
-        for i, gates in enumerate(near):
+        by_switch = [gates for gates in near if topo.same_plane(gates[0], leaves[0])]
+        by_cable = [gates for gates in near if not topo.same_plane(gates[0], leaves[0])]
+        few = len(leaves) // 4 if by_cable else len(leaves)
+        for gates in by_switch:
             for x in gates:
-                far_of[x] = leaves[i * share:(i + 1) * share]
+                far_of[x] = leaves[:few]
+        for gates in by_cable:
+            for x in gates:
+                far_of[x] = leaves[few:]
     return root, peers, near, far_of
 
 
@@ -75,81 +68,90 @@ def rank_program(g, core, T, topo):
         return
     sem = T.sem
     root, peers, near, far_of = _plan(T, topo)
-    arr = [sem["arr%d" % i] for i in range(NP)]
-    col = [T.kv[:, i * W:(i + 1) * W] for i in range(NP)]
+    ng = len(near[0])
+    w = 256 // ng
+
+    def place(half, j):
+        return T.kv[:, half * 256 + j * w:half * 256 + (j + 1) * w]
 
     out = _bits(topo.mask(root, near[0][0]))
     stay = [e for e in _bits(topo.mask(root, peers[0])) if e not in out]
-    nt = 2 * len(near)
-    root_eng = [out[j::nt] for j in range(nt)]
-    gate_far = [out[0::4], out[2::4]]
-    gate_on = out[1::2]
+    nt = ng * len(near)
+    root_eng = [out[t::nt] for t in range(nt)]
+
+    def gate_eng(x):
+        if len(far_of[x]) > 1:
+            return out, stay[0::2]
+        return out[0::2], out[1::2]
+
+    gsem, asem, own, ld = [sem.g0, sem.g1], [sem.a0, sem.a1], [sem.own0, sem.own1], [sem.ld0, sem.ld1]
+    queues = [g.sync, g.scalar]
 
     g.vector.memset(T.zero[:], 0.0).then_inc(sem.zs, 1)
     total = 0
     if core == root:
-        g.sync.dma_start(T.pd[0], T.k[:, 0:W]).then_inc(sem.ld0, 16)
-        g.scalar.dma_start(T.pd[1], T.k[:, W:2 * W]).then_inc(sem.ld0, 16)
-        g.sync.dma_start(T.pd[2], T.v[:, 0:W]).then_inc(sem.ld1, 16)
-        g.scalar.dma_start(T.pd[3], T.v[:, W:2 * W]).then_inc(sem.ld1, 16)
-        g.sync.dma_start(T.kv[:, 0:2 * W], T.k[:]).then_inc(sem.own0, 16)
-        g.scalar.dma_start(T.kv[:, 2 * W:4 * W], T.v[:]).then_inc(sem.own1, 16)
+        for half, x in ((0, T.k), (1, T.v)):
+            for j in range(ng):
+                queues[j % 2].dma_start(T.pd[half * ng + j], x[:, j * w:(j + 1) * w]).then_inc(ld[half], 16)
+        g.sync.dma_start(T.kv[:, 0:256], T.k[:]).then_inc(sem.own0, 16)
+        g.scalar.dma_start(T.kv[:, 256:512], T.v[:]).then_inc(sem.own1, 16)
         g.sync.dma_start(T.qs[:], T.q[:]).then_inc(sem.lq, 16)
-        for half, ld in ((0, sem.ld0), (1, sem.ld1)):
-            g.wait_ge(ld, 32)
+        for half in (0, 1):
+            g.wait_ge(ld[half], 16 * ng)
             transfers = []
-            for i in (2 * half, 2 * half + 1):
+            for j in range(ng):
                 for gates in near:
                     eng = root_eng[len(transfers)]
-                    transfers.append(_xfer(topo, core, [gates[i]], eng, arr[i], T.pd[i], T.pd[i]))
+                    blk = T.pd[half * ng + j]
+                    transfers.append(_xfer(topo, core, [gates[j]], eng, gsem[half], blk, blk))
                     total += len(eng)
             g.remote_dma_fused(transfers, local_sem=sem.sent)
         g.wait_ge(sem.own0, 16)
         g.wait_ge(sem.own1, 16)
-        g.remote_dma_fused([_xfer(topo, core, peers, stay, arr[0], T.kv[:], T.kv[:])], local_sem=sem.sent)
+        g.remote_dma_fused([_xfer(topo, core, peers, stay, sem.a0, T.kv[:], T.kv[:])], local_sem=sem.sent)
         total += len(stay)
-        ready = [(sem.own0, 16), (sem.own0, 16), (sem.own1, 16), (sem.own1, 16)]
+        ready = [[(own[0], 16)], [(own[1], 16)]]
     elif core in peers:
         g.sync.dma_start(T.qs[:], T.q[:]).then_inc(sem.lq, 16)
-        ready = [(arr[0], len(stay))] * NP
+        ready = [[(sem.a0, len(stay))], []]
     elif core in far_of:
         gates = [gs for gs in near if core in gs][0]
         me = gates.index(core)
         n = len(root_eng[0])
+        sibs = [c for c in gates if c != core]
+        e_far, e_on = gate_eng(core)
         g.sync.dma_start(T.qs[:], T.q[:]).then_inc(sem.lq, 16)
-        g.wait_ge(arr[me], n)
-        transfers = [_xfer(topo, core, [d], gate_far[j], arr[me], T.pd[me], col[me])
-                     for j, d in enumerate(far_of[core])]
-        transfers.append(_xfer(topo, core, [c for c in gates if c != core], gate_on, arr[me], T.pd[me], col[me]))
-        g.remote_dma_fused(transfers, local_sem=sem.sent)
-        total = sum(len(gate_far[j]) for j in range(len(far_of[core]))) + len(gate_on)
-        g.sync.wait_ge(arr[me], n)
-        g.sync.dma_start(col[me], T.pd[me]).then_inc(sem.own0, 16)
-        ready = [(arr[i], len(gate_on)) for i in range(NP)]
-        ready[me] = (sem.own0, 16)
+        for half in (0, 1):
+            blk = T.pd[half * ng + me]
+            g.wait_ge(gsem[half], n)
+            g.remote_dma_fused([_xfer(topo, core, far_of[core], e_far, asem[half], blk, place(half, me)),
+                                _xfer(topo, core, sibs, e_on, asem[half], blk, place(half, me))], local_sem=sem.sent)
+            total += len(e_far) + len(e_on)
+            queues[half].wait_ge(gsem[half], n)
+            queues[half].dma_start(place(half, me), blk).then_inc(own[half], 16)
+        ready = [[(own[half], 16), (asem[half], len(sibs) * len(e_on))] for half in (0, 1)]
     else:
-        feeders = [x for x in far_of if core in far_of[x]]
-        j = far_of[feeders[0]].index(core)
+        feeder = [x for x in far_of if core in far_of[x]][0]
         g.sync.dma_start(T.qs[:], T.q[:]).then_inc(sem.lq, 16)
-        ready = [(arr[i], len(gate_far[j])) for i in range(NP)]
+        ready = [[(asem[half], ng * len(gate_eng(feeder)[0]))] for half in (0, 1)]
 
     te, ve = g.tensor, g.vector
     te.wait_ge(sem.lq, 16)
-    te.wait_ge(ready[0][0], ready[0][1])
-    te.matmul(T.ps0[:, 0:256], col[0], T.qs[:], start=True, stop=True).then_inc(sem.mm0, 1)
-    te.wait_ge(ready[1][0], ready[1][1])
-    te.matmul(T.ps1[:, 0:256], col[1], T.qs[:], start=True, stop=True).then_inc(sem.mm1, 1)
+    for s, val in ready[0]:
+        te.wait_ge(s, val)
+    te.matmul(T.ps0[:, 0:256], T.kv[:, 0:128], T.qs[:], start=True, stop=True).then_inc(sem.mm0, 1)
+    te.matmul(T.ps1[:, 0:256], T.kv[:, 128:256], T.qs[:], start=True, stop=True).then_inc(sem.mm1, 1)
     ve.wait_ge(sem.zs, 1)
     ve.wait_ge(sem.mm0, 1)
     ve.tensor_tensor(T.s0[:], T.ps0[:, 0:256], T.zero[:], AluOpType.max).then_inc(sem.rl0, 1)
     ve.wait_ge(sem.mm1, 1)
     ve.tensor_tensor(T.s1[:], T.ps1[:, 0:256], T.zero[:], AluOpType.max).then_inc(sem.rl1, 1)
-    te.wait_ge(ready[2][0], ready[2][1])
+    for s, val in ready[1]:
+        te.wait_ge(s, val)
     te.wait_ge(sem.rl0, 1)
-    te.matmul(T.po[:, 0:256], col[2], T.s0[:], start=True, stop=False)
-    te.wait_ge(ready[3][0], ready[3][1])
+    te.matmul(T.po[:, 0:256], T.kv[:, 256:384], T.s0[:], start=True, stop=False)
     te.wait_ge(sem.rl1, 1)
-    te.matmul(T.po[:, 0:256], col[3], T.s1[:], start=False, stop=True).then_inc(sem.mo, 1)
+    te.matmul(T.po[:, 0:256], T.kv[:, 384:512], T.s1[:], start=False, stop=True).then_inc(sem.mo, 1)
     ve.wait_ge(sem.mo, 1)
     ve.tensor_copy(T.ys[:], T.po[:, 0:256]).then_inc(sem.cp, 1)
     g.sync.wait_ge(sem.cp, 1)

from concourse.bass import DstId, RemoteDMATransfer
from concourse.mybir import AluOpType

SCRATCH = {
    "pd": ("dram", [8, 128, 64], "bfloat16"),
    "kv": ("sbuf", [128, 512], "bfloat16"),
    "qs": ("sbuf", [128, 256], "bfloat16"),
    "zero": ("sbuf", [128, 256], "float32"),
    "s0": ("sbuf", [128, 256], "bfloat16"),
    "s1": ("sbuf", [128, 256], "bfloat16"),
    "ys": ("sbuf", [128, 256], "bfloat16"),
    "ps0": ("psum", [128, 512], "float32"),
    "ps1": ("psum", [128, 512], "float32"),
    "po": ("psum", [128, 512], "float32"),
}
SEMAPHORES = ["ld0", "ld1", "own0", "own1", "lq", "g0", "g1", "a0", "a1", "sent", "zs", "mm0", "mm1", "rl0", "rl1",
              "mo", "cp", "st"]


def _bits(mask):
    return [i for i in range(mask.bit_length()) if (mask >> i) & 1]


def _mask(engines):
    m = 0
    for e in engines:
        m |= 1 << e
    return m


def _plan(T, topo):
    cores = list(T.cores)
    root = cores[T.tables["MEM"][0]]
    by_host = {}
    for c in cores:
        by_host.setdefault(topo.host(c), []).append(c)
    peers = [c for c in by_host[topo.host(root)] if c != root]
    others = [h for h in by_host if h != topo.host(root)]
    near_h = [h for h in others if topo.may_write(root, by_host[h][0])]
    far_h = [h for h in others if h not in near_h]
    near = [by_host[h] for h in near_h]
    far_of = {x: [] for gates in near for x in gates}
    for h in far_h:
        leaves = by_host[h]
        by_switch = [gates for gates in near if topo.same_plane(gates[0], leaves[0])]
        by_cable = [gates for gates in near if not topo.same_plane(gates[0], leaves[0])]
        few = len(leaves) // 4 if by_cable else len(leaves)
        for gates in by_switch:
            for x in gates:
                far_of[x] = leaves[:few]
        for gates in by_cable:
            for x in gates:
                far_of[x] = leaves[few:]
    return root, peers, near, far_of


def _xfer(topo, core, dsts, engines, rsem, src, dst):
    ids = []
    for d in dsts:
        rid, pid = topo.addr(d, core)
        ids.append(DstId(rid=rid, pnc=pid))
    return RemoteDMATransfer(dst_ids=ids, dma_engine_mask=_mask(engines), remote_sem=rsem, srcs=[src],
                             dsts=[dst for d in dsts])


def rank_program(g, core, T, topo):
    if T.rank_of(core) is None:
        return
    sem = T.sem
    root, peers, near, far_of = _plan(T, topo)
    ng = len(near[0])
    w = 256 // ng

    def place(half, j):
        return T.kv[:, half * 256 + j * w:half * 256 + (j + 1) * w]

    out = _bits(topo.mask(root, near[0][0]))
    stay = [e for e in _bits(topo.mask(root, peers[0])) if e not in out]
    nt = ng * len(near)
    root_eng = [out[t::nt] for t in range(nt)]

    def gate_eng(x):
        if len(far_of[x]) > 1:
            return out, stay[0::2]
        return out[0::2], out[1::2]

    gsem, asem, own, ld = [sem.g0, sem.g1], [sem.a0, sem.a1], [sem.own0, sem.own1], [sem.ld0, sem.ld1]
    queues = [g.sync, g.scalar]

    g.vector.memset(T.zero[:], 0.0).then_inc(sem.zs, 1)
    total = 0
    if core == root:
        for half, x in ((0, T.k), (1, T.v)):
            for j in range(ng):
                queues[j % 2].dma_start(T.pd[half * ng + j], x[:, j * w:(j + 1) * w]).then_inc(ld[half], 16)
        g.sync.dma_start(T.kv[:, 0:256], T.k[:]).then_inc(sem.own0, 16)
        g.scalar.dma_start(T.kv[:, 256:512], T.v[:]).then_inc(sem.own1, 16)
        g.sync.dma_start(T.qs[:], T.q[:]).then_inc(sem.lq, 16)
        for half in (0, 1):
            g.wait_ge(ld[half], 16 * ng)
            transfers = []
            for j in range(ng):
                for gates in near:
                    eng = root_eng[len(transfers)]
                    blk = T.pd[half * ng + j]
                    transfers.append(_xfer(topo, core, [gates[j]], eng, gsem[half], blk, blk))
                    total += len(eng)
            g.remote_dma_fused(transfers, local_sem=sem.sent)
        g.wait_ge(sem.own0, 16)
        g.wait_ge(sem.own1, 16)
        g.remote_dma_fused([_xfer(topo, core, peers, stay, sem.a0, T.kv[:], T.kv[:])], local_sem=sem.sent)
        total += len(stay)
        ready = [[(own[0], 16)], [(own[1], 16)]]
    elif core in peers:
        g.sync.dma_start(T.qs[:], T.q[:]).then_inc(sem.lq, 16)
        ready = [[(sem.a0, len(stay))], []]
    elif core in far_of:
        gates = [gs for gs in near if core in gs][0]
        me = gates.index(core)
        n = len(root_eng[0])
        sibs = [c for c in gates if c != core]
        e_far, e_on = gate_eng(core)
        g.sync.dma_start(T.qs[:], T.q[:]).then_inc(sem.lq, 16)
        for half in (0, 1):
            blk = T.pd[half * ng + me]
            g.wait_ge(gsem[half], n)
            g.remote_dma_fused([_xfer(topo, core, far_of[core], e_far, asem[half], blk, place(half, me)),
                                _xfer(topo, core, sibs, e_on, asem[half], blk, place(half, me))], local_sem=sem.sent)
            total += len(e_far) + len(e_on)
            queues[half].wait_ge(gsem[half], n)
            queues[half].dma_start(place(half, me), blk).then_inc(own[half], 16)
        ready = [[(own[half], 16), (asem[half], len(sibs) * len(e_on))] for half in (0, 1)]
    else:
        feeder = [x for x in far_of if core in far_of[x]][0]
        g.sync.dma_start(T.qs[:], T.q[:]).then_inc(sem.lq, 16)
        ready = [[(asem[half], ng * len(gate_eng(feeder)[0]))] for half in (0, 1)]

    te, ve = g.tensor, g.vector
    te.wait_ge(sem.lq, 16)
    for s, val in ready[0]:
        te.wait_ge(s, val)
    te.matmul(T.ps0[:, 0:256], T.kv[:, 0:128], T.qs[:], start=True, stop=True).then_inc(sem.mm0, 1)
    te.matmul(T.ps1[:, 0:256], T.kv[:, 128:256], T.qs[:], start=True, stop=True).then_inc(sem.mm1, 1)
    ve.wait_ge(sem.zs, 1)
    ve.wait_ge(sem.mm0, 1)
    ve.tensor_tensor(T.s0[:], T.ps0[:, 0:256], T.zero[:], AluOpType.max).then_inc(sem.rl0, 1)
    ve.wait_ge(sem.mm1, 1)
    ve.tensor_tensor(T.s1[:], T.ps1[:, 0:256], T.zero[:], AluOpType.max).then_inc(sem.rl1, 1)
    for s, val in ready[1]:
        te.wait_ge(s, val)
    te.wait_ge(sem.rl0, 1)
    te.matmul(T.po[:, 0:256], T.kv[:, 256:384], T.s0[:], start=True, stop=False)
    te.wait_ge(sem.rl1, 1)
    te.matmul(T.po[:, 0:256], T.kv[:, 384:512], T.s1[:], start=False, stop=True).then_inc(sem.mo, 1)
    ve.wait_ge(sem.mo, 1)
    ve.tensor_copy(T.ys[:], T.po[:, 0:256]).then_inc(sem.cp, 1)
    g.sync.wait_ge(sem.cp, 1)
    g.sync.dma_start(T.y[:], T.ys[:]).then_inc(sem.st, 16)
    g.sync.wait_ge(sem.st, 16)
    if total:
        g.wait_ge(sem.sent, total)
